import numpy as np
import ml_dtypes


def mxq(x, axis, fmt="e4m3"):
    dtype, down = {"e4m3": (ml_dtypes.float8_e4m3fn, 7), "e5m2": (ml_dtypes.float8_e5m2, 14)}[fmt]
    v = np.moveaxis(np.asarray(x, np.float32).astype(ml_dtypes.bfloat16).astype(np.float64), axis, -1)
    blocks = v.reshape(v.shape[:-1] + (-1, 32))
    amax = np.abs(blocks).max(-1, keepdims=True)
    byte = np.maximum(np.where(amax > 0, np.frexp(amax)[1] - 1 + 127, 0) - down, 1)
    scale = np.exp2(byte - 127.0)
    codes = (blocks / scale).astype(np.float32).astype(dtype).astype(np.float64)
    return np.moveaxis((codes * scale).reshape(v.shape), -1, axis)


WIDE = False


def mx_kscale(k):
    if not WIDE:
        return np.ones(k)
    levels = np.array([10, -10, 5, -5, 0])
    if k % 512:
        return np.exp2(np.random.permutation(np.resize(levels, k // 32))).repeat(32)
    a = np.empty((k // 512, 16))
    for p in range(k // 512):
        a[p, :8] = np.random.permutation(np.resize(levels, 8))
        for g in range(8):
            far = levels[np.abs(levels - a[p, g]) >= 10]
            a[p, g + 8] = far[np.random.randint(len(far))]
    return np.exp2(a.ravel()).repeat(32)


def f64(x):
    return np.asarray(x).astype(np.float64)


def striped(idx):
    return np.tile(idx.reshape(-1, 16).T, (8, 1)).astype(np.uint16)


def unstriped(offs):
    return offs[:16].T.reshape(-1).astype(np.int64)


def pack_weight(w):
    k, n = w.shape
    w = f64(np.asarray(w, np.float32).astype(ml_dtypes.bfloat16)).reshape(k // 32, 32, n)
    amax = np.abs(w).max(1)
    byte = np.clip(np.where(amax > 0, np.frexp(amax)[1] - 1 + 127 - 7, 1), 1, 254)
    scaled = (w * np.exp2(127.0 - byte)[:, None, :]).reshape(k, n).astype(np.float32)
    words = np.ascontiguousarray(scaled.reshape(k // 512, 128, 4, n).transpose(0, 1, 3, 2)).astype(ml_dtypes.float8_e4m3fn).view(np.uint8)
    return words, np.ascontiguousarray(byte.astype(np.uint8).reshape(k // 512, 16, n))


def unpack_weight(words, scales):
    g, p, n, _ = words.shape
    vals = np.ascontiguousarray(words).view(ml_dtypes.float8_e4m3fn).astype(np.float64) * np.repeat(np.exp2(scales.astype(np.float64) - 127.0), 8, axis=1)[..., None]
    return vals.transpose(0, 1, 3, 2).reshape(g * 512, n)


def planes(y):
    n, m = y.shape
    v = y.astype(np.float32).astype(ml_dtypes.bfloat16).astype(np.float64).reshape(n // 32, 32, m)
    top = np.abs(v).max(1)
    byte = np.clip(np.where(top > 0, np.frexp(top)[1] - 1 + 127 - 7, 1), 1, 254)
    codes = (v * np.exp2(127.0 - byte)[:, None, :]).reshape(n, m).astype(np.float32).astype(ml_dtypes.float8_e4m3fn).view(np.uint8)
    words = codes.reshape(n // 512, 128, 4, m).transpose(0, 1, 3, 2)
    return np.ascontiguousarray(words), np.ascontiguousarray(byte.astype(np.uint8).reshape(n // 512, 16, m))


def relu(v):
    return np.maximum(v, 0.0)


K, T, S, D, V, N = 512, 2048, 1024, 2, 512, 512
P = 2 ** 7


def setup_inputs():
    n = np.random.standard_normal
    s = mx_kscale(K)[:, None]
    near = np.random.permutation(S)
    packed_xT = pack_weight(n((K, T)) * s)
    return {
        "x_words": packed_xT[0],
        "x_scales": packed_xT[1],
        "w1": (n((K, N)) / np.sqrt(K) / s).astype(np.float32),
        "w2": (n((K, N)) / np.sqrt(K) / s).astype(np.float32),
        "corr": (np.tile(np.random.uniform(0.0, 1.0, (4, 1, V)) / np.sqrt(D), (1, P, 1))).astype(np.float32),
        "offs": striped(np.random.permutation(T)[:S]),
        "pos1": striped(near[:V]),
        "pos2": striped(near[V:]),
    }


def reference(x_words, x_scales, w1, w2, corr, offs, pos1, pos2):
    xq = unpack_weight(x_words, x_scales)[:, unstriped(offs)]
    y0 = mxq(f64(w1), 0, "e4m3").T @ xq
    y1 = mxq(f64(w2), 0, "e4m3").T @ xq
    out_0 = relu(y0[:, unstriped(pos1)] * f64(corr)[0, :1] + y0[:, unstriped(pos2)] * f64(corr)[1, :1] + y1[:, unstriped(pos1)] * f64(corr)[2, :1] + y1[:, unstriped(pos2)] * f64(corr)[3, :1])
    return (out_0,) + planes(out_0)

@@ -1,0 +1,277 @@
+from contextlib import ExitStack
+
+import concourse.mybir as mybir
+from concourse.masks import make_identity
+
+K, T, S, V, N = 512, 2048, 1024, 512, 512
+FLOPS = 2 * 2 * K * N * S
+
+F32 = mybir.dt.float32
+BF16 = mybir.dt.bfloat16
+I32 = mybir.dt.int32
+U32 = mybir.dt.uint32
+U16 = mybir.dt.uint16
+U8 = mybir.dt.uint8
+FP8X4 = mybir.dt.float8_e4m3fn_x4
+ACT = mybir.ActivationFunctionType
+ALU = mybir.AluOpType
+
+P = 128
+PACK = 4
+BANK = 512
+HALF = N // 2
+PER_COLUMN = 16
+
+
+def tile_picked_zkp_relu_po_kernel(
+    tc, x_words, x_scales, w1, w2, corr, offs, pos1, pos2, out_0, out_1, out_2
+):
+    nc = tc.nc
+    with ExitStack() as ctx:
+        keep = ctx.enter_context(tc.tile_pool(name="keep", bufs=1))
+        psum = ctx.enter_context(tc.psum_pool(name="psum", bufs=1))
+
+        def bank_tile(bank, name):
+            return psum.tile([P, BANK], F32, name=name, tag=f"bank{bank}")
+
+        offs_sb = keep.tile([P, S // PER_COLUMN], U16, name="offs_sb")
+        pos_sb = [keep.tile([P, V // PER_COLUMN], U16, name=f"pos_sb{d}") for d in range(2)]
+        scale_table = keep.tile([P, T], U8, name="scale_table")
+        word_table = keep.tile([P, T], I32, name="word_table")
+        w_raw = [[keep.tile([P, PACK, HALF], F32, name=f"w_raw{q}{h}") for h in range(2)] for q in range(2)]
+        corr_sb = [keep.tile([P, V], F32, name=f"corr_sb{c}") for c in range(4)]
+        identity = keep.tile([P, P], F32, name="identity")
+
+        nc.gpsimd.memset(scale_table[:].bitcast(I32), 0)
+        make_identity(nc, identity[:])
+
+        def load_w(q, h):
+            rows = (w1, w2)[q].rearrange("(p j) m -> p j m", j=PACK)
+            nc.sync.dma_start(out=w_raw[q][h][:], in_=rows[:, :, h * HALF : (h + 1) * HALF])
+
+        def load_corr(c):
+            nc.sync.dma_start(out=corr_sb[c][:], in_=corr[c])
+
+        nc.sync.dma_start(offs_sb[:], offs)
+        for quad in range(4):
+            nc.sync.dma_start(
+                out=scale_table[32 * quad : 32 * quad + 4, :].bitcast(I32),
+                in_=x_scales[0, 4 * quad : 4 * quad + 4, :].bitcast(I32),
+            )
+        nc.sync.dma_start(out=word_table[:], in_=x_words[0].rearrange("p c r -> p (c r)").bitcast(I32))
+        load_w(0, 0)
+        load_w(1, 0)
+        nc.sync.dma_start(pos_sb[0][:], pos1)
+        load_corr(0)
+        nc.sync.dma_start(pos_sb[1][:], pos2)
+        load_w(0, 1)
+        load_corr(1)
+        load_w(1, 1)
+        load_corr(2)
+        load_corr(3)
+
+        x_bytes = keep.tile([P, S], U8, align_bytes=64, name="x_bytes")
+        nc.vector.tensor_copy(out=x_bytes[:], in_=scale_table[:].indirect(offs_sb[:]))
+        pieces = ((0, 512), (512, 768), (768, 1024))
+        x_codes = {}
+
+        def gather_words(a, b, tag):
+            x_codes[a] = keep.tile([P, b - a], U32, align_bytes=64, name=f"x_codes{a}", tag=tag)
+            nc.vector.tensor_copy(
+                out=x_codes[a][:],
+                in_=word_table[:].bitcast(U32).indirect(offs_sb[:, a // PER_COLUMN : b // PER_COLUMN]),
+            )
+
+        def quantize_w(grouped, width, name):
+            codes = keep.tile([P, width], U32, align_bytes=64, name=f"w_codes_{name}", tag=f"w_codes_{name}")
+            scales = keep.tile([P, width], U8, align_bytes=64, name=f"w_scales_{name}")
+            nc.vector.quantize_mx(out=codes[:].bitcast(FP8X4), scales=scales[:], in_=grouped[:])
+            return codes, scales
+
+        def round_low(q, h):
+            grouped = keep.tile([P, P * PACK], BF16, align_bytes=64, name=f"w_low{q}{h}", tag=f"w_low{q}{h}")
+            nc.scalar.activation(
+                out=grouped[:].rearrange("p (g t j) -> p g t j", t=2, j=PACK),
+                in_=w_raw[q][h][:].rearrange("p j (g t) -> p g t j", t=PACK)[:, :, 0:2, :],
+                func=ACT.Copy,
+            )
+            return grouped
+
+        def round_high(q):
+            grouped = keep.tile([P, 2 * P * PACK], BF16, align_bytes=64, name=f"w_high{q}", tag=f"w_high{q}")
+            dealt = grouped[:].rearrange("p (t g j) -> p g j t", t=2, j=PACK)
+            for h in range(2):
+                nc.scalar.copy(
+                    out=dealt[:, h * (P // 2) : (h + 1) * (P // 2), :, :],
+                    in_=w_raw[q][h][:].rearrange("p j (g t) -> p g j t", t=PACK)[:, :, :, 2:4],
+                )
+            return grouped
+
+        ys = {}
+
+        def product(block, q, weights, cols, banks):
+            codes, scales = weights
+            y = keep.tile([P, S], F32, name=f"y{block}{q}")
+            groups = [[piece] for piece in pieces] if len(banks) == 3 else [pieces[:1], pieces[1:]]
+            for group, bank in zip(groups, banks):
+                first, end = group[0][0], group[-1][1]
+                acc = bank_tile(bank, f"acc{block}{q}{first}")
+                for a, b in group:
+                    nc.tensor.matmul_mx(
+                        out=acc[:, a - first : b - first],
+                        lhsT=codes[:, cols].bitcast(FP8X4),
+                        lhsT_scale=scales[:, cols],
+                        rhs=x_codes[a][:].bitcast(FP8X4),
+                        rhs_scale=x_bytes[:, a:b],
+                        start=True,
+                        stop=True,
+                    )
+                nc.scalar.copy(out=y[:, first:end], in_=acc[:, : end - first])
+            ys[block, q] = y
+
+        def term(block, c, a, b, tag=None):
+            q, d = divmod(c, 2)
+            name = f"term{block}{c}_{a}"
+            weighted = keep.tile([P, b - a], F32, align_bytes=64, name=name, tag=tag or name)
+            nc.vector.tensor_tensor(
+                out=weighted[:],
+                in0=ys[block, q][:].indirect(pos_sb[d][:, a // PER_COLUMN : b // PER_COLUMN]),
+                in1=corr_sb[c][:, a:b],
+                op=ALU.mult,
+            )
+            return weighted
+
+        def sum_turned(four, strips, bank, name):
+            sums = bank_tile(bank, name)
+            for i in range(strips):
+                for c in range(4):
+                    nc.tensor.matmul(
+                        out=sums[:, i * P : (i + 1) * P],
+                        lhsT=four[c][:, i * P : (i + 1) * P],
+                        rhs=identity[:],
+                        is_transpose=True,
+                        start=(c == 0),
+                        stop=(c == 3),
+                    )
+            return sums
+
+        whole = slice(0, P)
+        upper = slice(P, 2 * P)
+
+        gather_words(*pieces[0], "x_codes0")
+        gather_words(*pieces[1], "x_codes1")
+        w00 = quantize_w(round_low(0, 0), P, "low00")
+        gather_words(*pieces[2], "w_low00")
+        w10 = quantize_w(round_low(1, 0), P, "low10")
+        product(0, 0, w00, whole, (0, 1, 2))
+        g01 = round_low(0, 1)
+        a0 = term(0, 0, 0, V)
+        w01 = quantize_w(g01, P, "low01")
+        product(0, 1, w10, whole, (3, 0))
+        g11 = round_low(1, 1)
+        a1 = term(0, 1, 0, V, "w_low01")
+        a2 = term(0, 2, 0, V)
+        w11 = quantize_w(g11, P, "low11")
+        product(1, 0, w01, whole, (1, 2))
+        gh0 = round_high(0)
+        a3 = term(0, 3, 0, V, "w_low11")
+        product(1, 1, w11, whole, (3, 0))
+        sums_a = sum_turned((a0, a1, a2, a3), 4, 3, "sums_a")
+        b0 = term(1, 0, 0, V)
+        wh0 = quantize_w(gh0, 2 * P, "high0")
+        gh1 = round_high(1)
+        b1 = term(1, 1, 0, V, "w_high0")
+        product(2, 0, wh0, whole, (1, 2))
+        b2 = term(1, 2, 0, V)
+        wh1 = quantize_w(gh1, 2 * P, "high1")
+        b3 = term(1, 3, 0, V, "w_high1")
+        product(3, 0, wh0, upper, (4, 5))
+        product(2, 1, wh1, whole, (6, 7))
+        product(3, 1, wh1, upper, (0, 1))
+        sums_b = sum_turned((b0, b1, b2, b3), 4, 5, "sums_b")
+
+        turned = keep.tile([P, V // P, PACK, P], F32, align_bytes=64, name="turned", tag="w_codes_high1")
+        for h, sums in enumerate((sums_a, sums_b)):
+            nc.scalar.activation(
+                out=turned[:, :, 0:2, h * (P // 2) : (h + 1) * (P // 2)],
+                in_=sums[:].rearrange("v (s g t) -> v s t g", s=V // P, t=2),
+                func=ACT.Relu,
+            )
+
+        out_rows = out_0.rearrange("(p t) v -> p t v", t=PACK)
+        out_codes = keep.tile([P, V], U32, align_bytes=64, name="out_codes")
+        out_scales = keep.tile([P, V], U8, align_bytes=64, name="out_scales")
+        out_words = out_1[0].rearrange("p c r -> p (c r)").bitcast(I32)
+
+        def quantize_out(rounded, s):
+            cols = slice(s * P, (s + 1) * P)
+            nc.vector.quantize_mx(
+                out=out_codes[:, cols].bitcast(FP8X4),
+                scales=out_scales[:, cols],
+                in_=rounded[:].rearrange("p v t -> p (v t)"),
+            )
+            nc.sync.dma_start(out=out_words[:, cols], in_=out_codes[:, cols].bitcast(I32))
+
+        def unit(t, s0, s1, bank, tag=None):
+            four = [term(t, c, s0 * P, s1 * P, tag if c == 0 else None) for c in range(4)]
+            sums = sum_turned(four, s1 - s0, bank, f"sums{t}{s0}")
+            nc.scalar.activation(
+                out=turned[:, s0:s1, t, :],
+                in_=sums[:, : (s1 - s0) * P].rearrange("v (s p) -> v s p", p=P),
+                func=ACT.Relu,
+            )
+
+        def turn_back(s, slots, bank):
+            back = bank_tile(bank, f"back{s}")[:].rearrange("p (t v) -> p t v", t=PACK)
+            for t in range(slots):
+                nc.tensor.transpose(back[:, t, :], turned[:, s, t, :], identity[:])
+            result = keep.tile([P, PACK, P], F32, name=f"result{s}")
+            return back, result
+
+        def finish(s, bank):
+            back, result = turn_back(s, PACK, bank)
+            rounded = keep.tile([P, P, PACK], BF16, align_bytes=64, name=f"rounded{s}", tag=f"rounded{s}")
+            nc.scalar.copy(out=rounded[:], in_=back.rearrange("p t v -> p v t"))
+            nc.scalar.copy(out=result[:], in_=back)
+            nc.sync.dma_start(out=out_rows[:, :, s * P : (s + 1) * P], in_=result[:])
+            return rounded
+
+        unit(2, 0, 2, 4)
+        unit(3, 0, 1, 6)
+        r0 = finish(0, 1)
+        unit(3, 1, 2, 4)
+        r1 = finish(1, 2)
+        unit(2, 2, 3, 6)
+        unit(3, 2, 3, 4)
+        r2 = finish(2, 7)
+        quantize_out(r0, 0)
+        unit(2, 3, 4, 6, "rounded0")
+        last_back, last_result = turn_back(3, PACK - 1, 0)
+        nc.scalar.copy(out=last_result[:, 0:3, :], in_=last_back[:, 0:3, :])
+        nc.sync.dma_start(out=out_rows[:, 0:3, 3 * P :], in_=last_result[:, 0:3, :])
+
+        d0 = term(3, 0, 3 * P, V)
+        quantize_out(r1, 1)
+        d1 = term(3, 1, 3 * P, V, "rounded1")
+        d2 = term(3, 2, 3 * P, V)
+        pair = keep.tile([P, P], F32, name="pair")
+        nc.vector.tensor_tensor(out=pair[:], in0=d0[:], in1=d1[:], op=ALU.add)
+        d3 = term(3, 3, 3 * P, V)
+        triple = keep.tile([P, P], F32, name="triple")
+        nc.vector.tensor_tensor(out=triple[:], in0=pair[:], in1=d2[:], op=ALU.add)
+        nc.vector.tensor_tensor(out=last_result[:, 3, :], in0=triple[:], in1=d3[:], op=ALU.add)
+        last_rounded = keep.tile([P, P, PACK], BF16, align_bytes=64, name="last_rounded")
+        nc.vector.tensor_scalar_max(
+            out=last_rounded[:], in0=last_result[:].rearrange("p t v -> p v t"), scalar1=0.0
+        )
+        quantize_out(r2, 2)
+        quantize_out(last_rounded, 3)
+        last_row = keep.tile([P, P], F32, name="last_row")
+        nc.scalar.activation(out=last_row[:], in_=last_result[:, 3, :], func=ACT.Relu)
+        nc.scalar.dma_start(out=out_rows[:, 3, 3 * P :], in_=last_row[:])
+        for quad in range(4):
+            queue = nc.sync if quad < 2 else nc.scalar
+            queue.dma_start(
+                out=out_2[0, 4 * quad : 4 * quad + 4, :].bitcast(I32),
+                in_=out_scales[32 * quad : 32 * quad + 4, :].bitcast(I32),
+            )

@@ -37,12 +37,12 @@ def tile_picked_zkp_relu_po_kernel(
         offs_sb = keep.tile([P, S // PER_COLUMN], U16, name="offs_sb")
         pos_sb = [keep.tile([P, V // PER_COLUMN], U16, name=f"pos_sb{d}") for d in range(2)]
         scale_table = keep.tile([P, T], U8, name="scale_table")
-        word_table = keep.tile([P, T], I32, name="word_table")
+        word_table = keep.tile([P, T], I32, align_bytes=64, name="word_table", tag="word_table")
         w_raw = [[keep.tile([P, PACK, HALF], F32, name=f"w_raw{q}{h}") for h in range(2)] for q in range(2)]
         corr_sb = [keep.tile([P, V], F32, name=f"corr_sb{c}") for c in range(4)]
         identity = keep.tile([P, P], F32, name="identity")
 
-        nc.gpsimd.memset(scale_table[:].bitcast(I32), 0)
+        nc.vector.memset(scale_table[:].bitcast(I32), 0)
         make_identity(nc, identity[:])
 
         def load_w(q, h):
@@ -53,6 +53,8 @@ def tile_picked_zkp_relu_po_kernel(
             nc.sync.dma_start(out=corr_sb[c][:], in_=corr[c])
 
         nc.sync.dma_start(offs_sb[:], offs)
+        nc.sync.dma_start(pos_sb[0][:], pos1)
+        nc.sync.dma_start(pos_sb[1][:], pos2)
         for quad in range(4):
             nc.sync.dma_start(
                 out=scale_table[32 * quad : 32 * quad + 4, :].bitcast(I32),
@@ -61,9 +63,7 @@ def tile_picked_zkp_relu_po_kernel(
         nc.sync.dma_start(out=word_table[:], in_=x_words[0].rearrange("p c r -> p (c r)").bitcast(I32))
         load_w(0, 0)
         load_w(1, 0)
-        nc.sync.dma_start(pos_sb[0][:], pos1)
         load_corr(0)
-        nc.sync.dma_start(pos_sb[1][:], pos2)
         load_w(0, 1)
         load_corr(1)
         load_w(1, 1)
@@ -84,28 +84,27 @@ def tile_picked_zkp_relu_po_kernel(
 
         def quantize_w(grouped, width, name):
             codes = keep.tile([P, width], U32, align_bytes=64, name=f"w_codes_{name}", tag=f"w_codes_{name}")
-            scales = keep.tile([P, width], U8, align_bytes=64, name=f"w_scales_{name}")
+            scales = keep.tile([P, width], U8, align_bytes=64, name=f"w_scales_{name}", tag=f"w_scales_{name}")
             nc.vector.quantize_mx(out=codes[:].bitcast(FP8X4), scales=scales[:], in_=grouped[:])
             return codes, scales
 
-        def round_low(q, h):
-            grouped = keep.tile([P, P * PACK], BF16, align_bytes=64, name=f"w_low{q}{h}", tag=f"w_low{q}{h}")
-            nc.scalar.activation(
-                out=grouped[:].rearrange("p (g t j) -> p g t j", t=2, j=PACK),
-                in_=w_raw[q][h][:].rearrange("p j (g t) -> p g t j", t=PACK)[:, :, 0:2, :],
-                func=ACT.Copy,
+        def round_low(q, h, copy, tag=None):
+            grouped = keep.tile([P, P * PACK], BF16, align_bytes=64, name=f"w_low{q}{h}", tag=tag or f"w_low{q}{h}")
+            copy(
+                out=grouped[:].rearrange("p (g t j) -> p g j t", t=2, j=PACK),
+                in_=w_raw[q][h][:].rearrange("p j (g t) -> p g j t", t=PACK)[:, :, :, 0:2],
             )
             return grouped
 
-        def round_high(q):
-            grouped = keep.tile([P, 2 * P * PACK], BF16, align_bytes=64, name=f"w_high{q}", tag=f"w_high{q}")
-            dealt = grouped[:].rearrange("p (t g j) -> p g j t", t=2, j=PACK)
-            for h in range(2):
-                nc.scalar.copy(
-                    out=dealt[:, h * (P // 2) : (h + 1) * (P // 2), :, :],
-                    in_=w_raw[q][h][:].rearrange("p j (g t) -> p g j t", t=PACK)[:, :, :, 2:4],
-                )
-            return grouped
+        def scalar_cast(out, in_):
+            nc.scalar.activation(out=out, in_=in_, func=ACT.Copy)
+
+        def round_high(q, h):
+            dealt = w_high[q][:].rearrange("p (t g j) -> p g j t", t=2, j=PACK)
+            nc.scalar.copy(
+                out=dealt[:, h * (P // 2) : (h + 1) * (P // 2), :, :],
+                in_=w_raw[q][h][:].rearrange("p j (g t) -> p g j t", t=PACK)[:, :, :, 2:4],
+            )
 
         ys = {}
 
@@ -160,31 +159,37 @@ def tile_picked_zkp_relu_po_kernel(
 
         gather_words(*pieces[0], "x_codes0")
         gather_words(*pieces[1], "x_codes1")
-        w00 = quantize_w(round_low(0, 0), P, "low00")
+        w00 = quantize_w(round_low(0, 0, scalar_cast), P, "low00")
         gather_words(*pieces[2], "w_low00")
-        w10 = quantize_w(round_low(1, 0), P, "low10")
+        w10 = quantize_w(round_low(1, 0, nc.vector.tensor_copy, "word_table"), P, "low10")
         product(0, 0, w00, whole, (0, 1, 2))
-        g01 = round_low(0, 1)
         a0 = term(0, 0, 0, V)
-        w01 = quantize_w(g01, P, "low01")
         product(0, 1, w10, whole, (3, 0))
-        g11 = round_low(1, 1)
-        a1 = term(0, 1, 0, V, "w_low01")
-        a2 = term(0, 2, 0, V)
+        w_high = [
+            keep.tile([P, 2 * P * PACK], BF16, align_bytes=64, name=f"w_high{q}", tag=f"w_codes_low{q}0")
+            for q in range(2)
+        ]
+        g01 = round_low(0, 1, scalar_cast, "w_scales_low00")
+        a1 = term(0, 1, 0, V)
+        w01 = quantize_w(g01, P, "low01")
+        g11 = round_low(1, 1, scalar_cast, "w_scales_low10")
+        a2 = term(0, 2, 0, V, "w_scales_low00")
         w11 = quantize_w(g11, P, "low11")
         product(1, 0, w01, whole, (1, 2))
-        gh0 = round_high(0)
-        a3 = term(0, 3, 0, V, "w_low11")
+        round_high(0, 0)
+        round_high(0, 1)
+        a3 = term(0, 3, 0, V, "w_scales_low10")
         product(1, 1, w11, whole, (3, 0))
         sums_a = sum_turned((a0, a1, a2, a3), 4, 3, "sums_a")
         b0 = term(1, 0, 0, V)
-        wh0 = quantize_w(gh0, 2 * P, "high0")
-        gh1 = round_high(1)
-        b1 = term(1, 1, 0, V, "w_high0")
+        wh0 = quantize_w(w_high[0], 2 * P, "high0")
+        round_high(1, 0)
+        round_high(1, 1)
+        b1 = term(1, 1, 0, V, "w_codes_low00")
         product(2, 0, wh0, whole, (1, 2))
-        b2 = term(1, 2, 0, V)
-        wh1 = quantize_w(gh1, 2 * P, "high1")
-        b3 = term(1, 3, 0, V, "w_high1")
+        wh1 = quantize_w(w_high[1], 2 * P, "high1")
+        b2 = term(1, 2, 0, V, "w_codes_low10")
+        b3 = term(1, 3, 0, V)
         product(3, 0, wh0, upper, (4, 5))
         product(2, 1, wh1, whole, (6, 7))
         product(3, 1, wh1, upper, (0, 1))
@@ -237,6 +242,9 @@ def tile_picked_zkp_relu_po_kernel(
             return rounded
 
         unit(2, 0, 2, 4)
+        last_back, last_result = turn_back(3, 2, 0)
+        nc.scalar.copy(out=last_result[:, 0:2, :], in_=last_back[:, 0:2, :])
+        nc.sync.dma_start(out=out_rows[:, 0:2, 3 * P :], in_=last_result[:, 0:2, :])
         unit(3, 0, 1, 6)
         r0 = finish(0, 1)
         unit(3, 1, 2, 4)
@@ -244,31 +252,36 @@ def tile_picked_zkp_relu_po_kernel(
         unit(2, 2, 3, 6)
         unit(3, 2, 3, 4)
         r2 = finish(2, 7)
-        quantize_out(r0, 0)
-        unit(2, 3, 4, 6, "rounded0")
-        last_back, last_result = turn_back(3, PACK - 1, 0)
-        nc.scalar.copy(out=last_result[:, 0:3, :], in_=last_back[:, 0:3, :])
-        nc.sync.dma_start(out=out_rows[:, 0:3, 3 * P :], in_=last_result[:, 0:3, :])
 
-        d0 = term(3, 0, 3 * P, V)
+        def add(out, in0, in1):
+            nc.vector.tensor_tensor(out=out, in0=in0, in1=in1, op=ALU.add)
+
+        partial = keep.tile([P, 4, P], F32, name="partial")
+        last_rows = keep.tile([P, 2, P], F32, name="last_rows")
+        quantize_out(r0, 0)
+        c0 = term(2, 0, 3 * P, V, "rounded0")
+        c1 = term(2, 1, 3 * P, V)
+        c2 = term(2, 2, 3 * P, V)
+        add(partial[:, 0, :], c0[:], c1[:])
+        c3 = term(2, 3, 3 * P, V)
+        add(partial[:, 1, :], partial[:, 0, :], c2[:])
         quantize_out(r1, 1)
-        d1 = term(3, 1, 3 * P, V, "rounded1")
+        d0 = term(3, 0, 3 * P, V, "rounded1")
+        add(last_result[:, 2, :], partial[:, 1, :], c3[:])
+        d1 = term(3, 1, 3 * P, V)
         d2 = term(3, 2, 3 * P, V)
-        pair = keep.tile([P, P], F32, name="pair")
-        nc.vector.tensor_tensor(out=pair[:], in0=d0[:], in1=d1[:], op=ALU.add)
+        add(partial[:, 2, :], d0[:], d1[:])
         d3 = term(3, 3, 3 * P, V)
-        triple = keep.tile([P, P], F32, name="triple")
-        nc.vector.tensor_tensor(out=triple[:], in0=pair[:], in1=d2[:], op=ALU.add)
-        nc.vector.tensor_tensor(out=last_result[:, 3, :], in0=triple[:], in1=d3[:], op=ALU.add)
+        add(partial[:, 3, :], partial[:, 2, :], d2[:])
+        add(last_result[:, 3, :], partial[:, 3, :], d3[:])
         last_rounded = keep.tile([P, P, PACK], BF16, align_bytes=64, name="last_rounded")
         nc.vector.tensor_scalar_max(
             out=last_rounded[:], in0=last_result[:].rearrange("p t v -> p v t"), scalar1=0.0
         )
         quantize_out(r2, 2)
         quantize_out(last_rounded, 3)
-        last_row = keep.tile([P, P], F32, name="last_row")
-        nc.scalar.activation(out=last_row[:], in_=last_result[:, 3, :], func=ACT.Relu)
-        nc.scalar.dma_start(out=out_rows[:, 3, 3 * P :], in_=last_row[:])
+        nc.scalar.activation(out=last_rows[:], in_=last_result[:, 2:4, :], func=ACT.Relu)
+        nc.scalar.dma_start(out=out_rows[:, 2:4, 3 * P :], in_=last_rows[:])
         for quad in range(4):
             queue = nc.sync if quad < 2 else nc.scalar
             queue.dma_start(

@@ -125,20 +125,25 @@ def tile_picked_zkp_relu_po_kernel(
                         start=True,
                         stop=True,
                     )
-                nc.scalar.copy(out=y[:, first:end], in_=acc[:, : end - first])
+                copy = nc.vector.tensor_copy if len(banks) == 3 and first == pieces[1][0] else nc.scalar.copy
+                copy(out=y[:, first:end], in_=acc[:, : end - first])
             ys[block, q] = y
 
-        def term(block, c, a, b, tag=None):
+        def term(block, c, a, b, tag=None, into=None):
             q, d = divmod(c, 2)
             name = f"term{block}{c}_{a}"
-            weighted = keep.tile([P, b - a], F32, align_bytes=64, name=name, tag=tag or name)
+            if into is None:
+                into = keep.tile([P, b - a], F32, align_bytes=64, name=name, tag=tag or name)[:]
             nc.vector.tensor_tensor(
-                out=weighted[:],
+                out=into,
                 in0=ys[block, q][:].indirect(pos_sb[d][:, a // PER_COLUMN : b // PER_COLUMN]),
                 in1=corr_sb[c][:, a:b],
                 op=ALU.mult,
             )
-            return weighted
+            return into
+
+        def spent(c, s):
+            return corr_sb[c][:, s * P : (s + 1) * P]
 
         def sum_turned(four, strips, bank, name):
             sums = bank_tile(bank, name)
@@ -163,35 +168,34 @@ def tile_picked_zkp_relu_po_kernel(
         gather_words(*pieces[2], "w_low00")
         w10 = quantize_w(round_low(1, 0, nc.vector.tensor_copy, "word_table"), P, "low10")
         product(0, 0, w00, whole, (0, 1, 2))
-        a0 = term(0, 0, 0, V)
-        product(0, 1, w10, whole, (3, 0))
-        w_high = [
-            keep.tile([P, 2 * P * PACK], BF16, align_bytes=64, name=f"w_high{q}", tag=f"w_codes_low{q}0")
-            for q in range(2)
-        ]
         g01 = round_low(0, 1, scalar_cast, "w_scales_low00")
-        a1 = term(0, 1, 0, V)
+        a0 = term(0, 0, 0, V)
         w01 = quantize_w(g01, P, "low01")
+        product(0, 1, w10, whole, (3, 0))
         g11 = round_low(1, 1, scalar_cast, "w_scales_low10")
-        a2 = term(0, 2, 0, V, "w_scales_low00")
+        a1 = term(0, 1, 0, V, "w_scales_low00")
+        a2 = term(0, 2, 0, V)
         w11 = quantize_w(g11, P, "low11")
         product(1, 0, w01, whole, (1, 2))
-        round_high(0, 0)
-        round_high(0, 1)
         a3 = term(0, 3, 0, V, "w_scales_low10")
         product(1, 1, w11, whole, (3, 0))
         sums_a = sum_turned((a0, a1, a2, a3), 4, 3, "sums_a")
+        w_high = [
+            keep.tile([P, 2 * P * PACK], BF16, align_bytes=64, name=f"w_high{q}", tag=f"w_codes_low{q}1")
+            for q in range(2)
+        ]
+        for q in range(2):
+            for h in range(2):
+                round_high(q, h)
         b0 = term(1, 0, 0, V)
+        b1 = term(1, 1, 0, V)
         wh0 = quantize_w(w_high[0], 2 * P, "high0")
-        round_high(1, 0)
-        round_high(1, 1)
-        b1 = term(1, 1, 0, V, "w_codes_low00")
-        product(2, 0, wh0, whole, (1, 2))
+        b2 = term(1, 2, 0, V, "w_codes_low01")
         wh1 = quantize_w(w_high[1], 2 * P, "high1")
-        b2 = term(1, 2, 0, V, "w_codes_low10")
-        b3 = term(1, 3, 0, V)
-        product(3, 0, wh0, upper, (4, 5))
-        product(2, 1, wh1, whole, (6, 7))
+        b3 = term(1, 3, 0, V, "w_codes_low11")
+        product(2, 0, wh0, whole, (1, 2))
+        product(2, 1, wh1, whole, (4, 5))
+        product(3, 0, wh0, upper, (6, 7))
         product(3, 1, wh1, upper, (0, 1))
         sums_b = sum_turned((b0, b1, b2, b3), 4, 5, "sums_b")
 
@@ -208,23 +212,32 @@ def tile_picked_zkp_relu_po_kernel(
         out_scales = keep.tile([P, V], U8, align_bytes=64, name="out_scales")
         out_words = out_1[0].rearrange("p c r -> p (c r)").bitcast(I32)
 
-        def quantize_out(rounded, s):
-            cols = slice(s * P, (s + 1) * P)
+        def quantize_out(rounded, s0, s1):
+            cols = slice(s0 * P, s1 * P)
             nc.vector.quantize_mx(
                 out=out_codes[:, cols].bitcast(FP8X4),
                 scales=out_scales[:, cols],
-                in_=rounded[:].rearrange("p v t -> p (v t)"),
+                in_=rounded.rearrange("p v t -> p (v t)"),
             )
-            nc.sync.dma_start(out=out_words[:, cols], in_=out_codes[:, cols].bitcast(I32))
 
-        def unit(t, s0, s1, bank, tag=None):
-            four = [term(t, c, s0 * P, s1 * P, tag if c == 0 else None) for c in range(4)]
-            sums = sum_turned(four, s1 - s0, bank, f"sums{t}{s0}")
-            nc.scalar.activation(
-                out=turned[:, s0:s1, t, :],
-                in_=sums[:, : (s1 - s0) * P].rearrange("v (s p) -> v s p", p=P),
-                func=ACT.Relu,
+        def rectify(t, s, sums):
+            nc.scalar.activation(out=turned[:, s, t, :], in_=sums[:, :P], func=ACT.Relu)
+
+        def add_turned(sums, weighted, c):
+            nc.tensor.matmul(
+                out=sums[:, :P], lhsT=weighted, rhs=identity[:], is_transpose=True, start=(c == 0), stop=(c == 3)
             )
+
+        def unit(t, s0, banks):
+            strips = range(len(banks))
+            sums = [bank_tile(banks[i], f"sums{t}{s0 + i}") for i in strips]
+            for c in range(4):
+                into = spent(c + 2, s0 - 1) if s0 > 0 and c < 2 else None
+                weighted = term(t, c, s0 * P, (s0 + len(banks)) * P, into=into)
+                for i in strips:
+                    add_turned(sums[i], weighted[:, i * P : (i + 1) * P], c)
+            for i in strips:
+                rectify(t, s0 + i, sums[i])
 
         def turn_back(s, slots, bank):
             back = bank_tile(bank, f"back{s}")[:].rearrange("p (t v) -> p t v", t=PACK)
@@ -233,55 +246,55 @@ def tile_picked_zkp_relu_po_kernel(
             result = keep.tile([P, PACK, P], F32, name=f"result{s}")
             return back, result
 
-        def finish(s, bank):
+        def finish(s, bank, rounded):
             back, result = turn_back(s, PACK, bank)
-            rounded = keep.tile([P, P, PACK], BF16, align_bytes=64, name=f"rounded{s}", tag=f"rounded{s}")
-            nc.scalar.copy(out=rounded[:], in_=back.rearrange("p t v -> p v t"))
+            nc.scalar.copy(out=rounded, in_=back.rearrange("p t v -> p v t"))
             nc.scalar.copy(out=result[:], in_=back)
             nc.sync.dma_start(out=out_rows[:, :, s * P : (s + 1) * P], in_=result[:])
-            return rounded
 
-        unit(2, 0, 2, 4)
-        last_back, last_result = turn_back(3, 2, 0)
+        rounded01 = keep.tile([P, 2 * P, PACK], BF16, align_bytes=64, name="rounded01", tag="rounded01")
+        rounded2 = keep.tile([P, P, PACK], BF16, align_bytes=64, name="rounded2", tag="rounded2")
+        unit(2, 0, (6, 7, 0))
+        last_back, last_result = turn_back(3, 2, 4)
         nc.scalar.copy(out=last_result[:, 0:2, :], in_=last_back[:, 0:2, :])
         nc.sync.dma_start(out=out_rows[:, 0:2, 3 * P :], in_=last_result[:, 0:2, :])
-        unit(3, 0, 1, 6)
-        r0 = finish(0, 1)
-        unit(3, 1, 2, 4)
-        r1 = finish(1, 2)
-        unit(2, 2, 3, 6)
-        unit(3, 2, 3, 4)
-        r2 = finish(2, 7)
+        unit(3, 0, (3,))
+        finish(0, 1, rounded01[:, :P, :])
+        unit(3, 1, (5,))
+        finish(1, 2, rounded01[:, P:, :])
+        unit(3, 2, (3,))
+        finish(2, 4, rounded2[:])
 
         def add(out, in0, in1):
             nc.vector.tensor_tensor(out=out, in0=in0, in1=in1, op=ALU.add)
 
-        partial = keep.tile([P, 4, P], F32, name="partial")
-        last_rows = keep.tile([P, 2, P], F32, name="last_rows")
-        quantize_out(r0, 0)
-        c0 = term(2, 0, 3 * P, V, "rounded0")
-        c1 = term(2, 1, 3 * P, V)
-        c2 = term(2, 2, 3 * P, V)
-        add(partial[:, 0, :], c0[:], c1[:])
-        c3 = term(2, 3, 3 * P, V)
-        add(partial[:, 1, :], partial[:, 0, :], c2[:])
-        quantize_out(r1, 1)
-        d0 = term(3, 0, 3 * P, V, "rounded1")
-        add(last_result[:, 2, :], partial[:, 1, :], c3[:])
-        d1 = term(3, 1, 3 * P, V)
+        partial = keep.tile([P, 3, P], F32, name="partial")
+        c0 = term(2, 0, 3 * P, V, into=spent(2, 2))
+        c1 = term(2, 1, 3 * P, V, into=spent(3, 2))
+        c2 = term(2, 2, 3 * P, V, into=spent(0, 1))
+        add(partial[:, 0, :], c0, c1)
+        c3 = term(2, 3, 3 * P, V, into=spent(1, 1))
+        add(partial[:, 1, :], partial[:, 0, :], c2)
+        d0 = term(3, 0, 3 * P, V, into=spent(1, 2))
+        add(last_result[:, 2, :], partial[:, 1, :], c3)
+        d1 = term(3, 1, 3 * P, V, into=spent(0, 2))
         d2 = term(3, 2, 3 * P, V)
-        add(partial[:, 2, :], d0[:], d1[:])
+        add(partial[:, 2, :], d0, d1)
         d3 = term(3, 3, 3 * P, V)
-        add(partial[:, 3, :], partial[:, 2, :], d2[:])
-        add(last_result[:, 3, :], partial[:, 3, :], d3[:])
-        last_rounded = keep.tile([P, P, PACK], BF16, align_bytes=64, name="last_rounded")
-        nc.vector.tensor_scalar_max(
-            out=last_rounded[:], in0=last_result[:].rearrange("p t v -> p v t"), scalar1=0.0
-        )
-        quantize_out(r2, 2)
-        quantize_out(last_rounded, 3)
-        nc.scalar.activation(out=last_rows[:], in_=last_result[:, 2:4, :], func=ACT.Relu)
-        nc.scalar.dma_start(out=out_rows[:, 2:4, 3 * P :], in_=last_rows[:])
+        quantize_out(rounded01[:], 0, 2)
+        nc.sync.dma_start(out=out_words[:, : 2 * P], in_=out_codes[:, : 2 * P].bitcast(I32))
+        triple = keep.tile([P, P], F32, align_bytes=64, name="triple", tag="rounded01")
+        add(triple[:], partial[:, 2, :], d2)
+        add(last_result[:, 3, :], triple[:], d3)
+        quantize_out(rounded2[:], 2, 3)
+        last = keep.tile([P, 2, P * PACK], BF16, align_bytes=64, name="last", tag="rounded2")
+        last_rounded = last[:, 0, :].rearrange("p (v t) -> p v t", t=PACK)
+        last_rows = last[:, 1, :].bitcast(F32).rearrange("p (t v) -> p t v", t=2)
+        nc.vector.tensor_scalar_max(out=last_rounded, in0=last_result[:].rearrange("p t v -> p v t"), scalar1=0.0)
+        nc.scalar.activation(out=last_rows, in_=last_result[:, 2:4, :], func=ACT.Relu)
+        nc.scalar.dma_start(out=out_rows[:, 2:4, 3 * P :], in_=last_rows)
+        quantize_out(last_rounded, 3, 4)
+        nc.sync.dma_start(out=out_words[:, 2 * P :], in_=out_codes[:, 2 * P :].bitcast(I32))
         for quad in range(4):
             queue = nc.sync if quad < 2 else nc.scalar
             queue.dma_start(

@@ -54,7 +54,6 @@ def tile_picked_zkp_relu_po_kernel(
 
         nc.sync.dma_start(offs_sb[:], offs)
         nc.sync.dma_start(pos_sb[0][:], pos1)
-        nc.sync.dma_start(pos_sb[1][:], pos2)
         for quad in range(4):
             nc.sync.dma_start(
                 out=scale_table[32 * quad : 32 * quad + 4, :].bitcast(I32),
@@ -64,6 +63,7 @@ def tile_picked_zkp_relu_po_kernel(
         load_w(0, 0)
         load_w(1, 0)
         load_corr(0)
+        nc.sync.dma_start(pos_sb[1][:], pos2)
         load_w(0, 1)
         load_corr(1)
         load_w(1, 1)
@@ -168,16 +168,16 @@ def tile_picked_zkp_relu_po_kernel(
         gather_words(*pieces[2], "w_low00")
         w10 = quantize_w(round_low(1, 0, nc.vector.tensor_copy, "word_table"), P, "low10")
         product(0, 0, w00, whole, (0, 1, 2))
-        g01 = round_low(0, 1, scalar_cast, "w_scales_low00")
         a0 = term(0, 0, 0, V)
-        w01 = quantize_w(g01, P, "low01")
         product(0, 1, w10, whole, (3, 0))
+        g01 = round_low(0, 1, scalar_cast, "w_scales_low00")
         g11 = round_low(1, 1, scalar_cast, "w_scales_low10")
-        a1 = term(0, 1, 0, V, "w_scales_low00")
-        a2 = term(0, 2, 0, V)
-        w11 = quantize_w(g11, P, "low11")
+        a1 = term(0, 1, 0, V)
+        w01 = quantize_w(g01, P, "low01")
+        a2 = term(0, 2, 0, V, "w_scales_low00")
         product(1, 0, w01, whole, (1, 2))
-        a3 = term(0, 3, 0, V, "w_scales_low10")
+        a3 = term(0, 3, 0, V)
+        w11 = quantize_w(g11, P, "low11")
         product(1, 1, w11, whole, (3, 0))
         sums_a = sum_turned((a0, a1, a2, a3), 4, 3, "sums_a")
         w_high = [
@@ -187,7 +187,7 @@ def tile_picked_zkp_relu_po_kernel(
         for q in range(2):
             for h in range(2):
                 round_high(q, h)
-        b0 = term(1, 0, 0, V)
+        b0 = term(1, 0, 0, V, "w_scales_low10")
         b1 = term(1, 1, 0, V)
         wh0 = quantize_w(w_high[0], 2 * P, "high0")
         b2 = term(1, 2, 0, V, "w_codes_low01")

from contextlib import ExitStack

import concourse.mybir as mybir
from concourse.masks import make_identity

K, T, S, V, N = 512, 2048, 1024, 512, 512
FLOPS = 2 * 2 * K * N * S

F32 = mybir.dt.float32
BF16 = mybir.dt.bfloat16
I32 = mybir.dt.int32
U32 = mybir.dt.uint32
U16 = mybir.dt.uint16
U8 = mybir.dt.uint8
FP8X4 = mybir.dt.float8_e4m3fn_x4
ACT = mybir.ActivationFunctionType
ALU = mybir.AluOpType

P = 128
PACK = 4
BANK = 512
HALF = N // 2
PER_COLUMN = 16


def tile_picked_zkp_relu_po_kernel(
    tc, x_words, x_scales, w1, w2, corr, offs, pos1, pos2, out_0, out_1, out_2
):
    nc = tc.nc
    with ExitStack() as ctx:
        keep = ctx.enter_context(tc.tile_pool(name="keep", bufs=1))
        psum = ctx.enter_context(tc.psum_pool(name="psum", bufs=1))

        def bank_tile(bank, name):
            return psum.tile([P, BANK], F32, name=name, tag=f"bank{bank}")

        offs_sb = keep.tile([P, S // PER_COLUMN], U16, name="offs_sb")
        pos_sb = [keep.tile([P, V // PER_COLUMN], U16, name=f"pos_sb{d}") for d in range(2)]
        scale_table = keep.tile([P, T], U8, name="scale_table")
        word_table = keep.tile([P, T], I32, align_bytes=64, name="word_table", tag="word_table")
        w_raw = [[keep.tile([P, PACK, HALF], F32, name=f"w_raw{q}{h}") for h in range(2)] for q in range(2)]
        corr_sb = [keep.tile([P, V], F32, name=f"corr_sb{c}") for c in range(4)]
        identity = keep.tile([P, P], F32, name="identity")

        nc.vector.memset(scale_table[:].bitcast(I32), 0)
        make_identity(nc, identity[:])

        def load_w(q, h):
            rows = (w1, w2)[q].rearrange("(p j) m -> p j m", j=PACK)
            nc.sync.dma_start(out=w_raw[q][h][:], in_=rows[:, :, h * HALF : (h + 1) * HALF])

        def load_corr(c):
            nc.sync.dma_start(out=corr_sb[c][:], in_=corr[c])

        nc.sync.dma_start(offs_sb[:], offs)
        nc.sync.dma_start(pos_sb[0][:], pos1)
        for quad in range(4):
            nc.sync.dma_start(
                out=scale_table[32 * quad : 32 * quad + 4, :].bitcast(I32),
                in_=x_scales[0, 4 * quad : 4 * quad + 4, :].bitcast(I32),
            )
        nc.sync.dma_start(out=word_table[:], in_=x_words[0].rearrange("p c r -> p (c r)").bitcast(I32))
        load_w(0, 0)
        load_w(1, 0)
        load_corr(0)
        nc.sync.dma_start(pos_sb[1][:], pos2)
        load_w(0, 1)
        load_corr(1)
        load_w(1, 1)
        load_corr(2)
        load_corr(3)

        x_bytes = keep.tile([P, S], U8, align_bytes=64, name="x_bytes")
        nc.vector.tensor_copy(out=x_bytes[:], in_=scale_table[:].indirect(offs_sb[:]))
        pieces = ((0, 512), (512, 768), (768, 1024))
        x_codes = {}

        def gather_words(a, b, tag):
            x_codes[a] = keep.tile([P, b - a], U32, align_bytes=64, name=f"x_codes{a}", tag=tag)
            nc.vector.tensor_copy(
                out=x_codes[a][:],
                in_=word_table[:].bitcast(U32).indirect(offs_sb[:, a // PER_COLUMN : b // PER_COLUMN]),
            )

        def quantize_w(grouped, width, name):
            codes = keep.tile([P, width], U32, align_bytes=64, name=f"w_codes_{name}", tag=f"w_codes_{name}")
            scales = keep.tile([P, width], U8, align_bytes=64, name=f"w_scales_{name}", tag=f"w_scales_{name}")
            nc.vector.quantize_mx(out=codes[:].bitcast(FP8X4), scales=scales[:], in_=grouped[:])
            return codes, scales

        def round_low(q, h, copy, tag=None):
            grouped = keep.tile([P, P * PACK], BF16, align_bytes=64, name=f"w_low{q}{h}", tag=tag or f"w_low{q}{h}")
            copy(
                out=grouped[:].rearrange("p (g t j) -> p g j t", t=2, j=PACK),
                in_=w_raw[q][h][:].rearrange("p j (g t) -> p g j t", t=PACK)[:, :, :, 0:2],
            )
            return grouped

        def scalar_cast(out, in_):
            nc.scalar.activation(out=out, in_=in_, func=ACT.Copy)

        def round_high(q, h):
            dealt = w_high[q][:].rearrange("p (t g j) -> p g j t", t=2, j=PACK)
            nc.scalar.copy(
                out=dealt[:, h * (P // 2) : (h + 1) * (P // 2), :, :],
                in_=w_raw[q][h][:].rearrange("p j (g t) -> p g j t", t=PACK)[:, :, :, 2:4],
            )

        ys = {}

        def product(block, q, weights, cols, banks):
            codes, scales = weights
            y = keep.tile([P, S], F32, name=f"y{block}{q}")
            groups = [[piece] for piece in pieces] if len(banks) == 3 else [pieces[:1], pieces[1:]]
            for group, bank in zip(groups, banks):
                first, end = group[0][0], group[-1][1]
                acc = bank_tile(bank, f"acc{block}{q}{first}")
                for a, b in group:
                    nc.tensor.matmul_mx(
                        out=acc[:, a - first : b - first],
                        lhsT=codes[:, cols].bitcast(FP8X4),
                        lhsT_scale=scales[:, cols],
                        rhs=x_codes[a][:].bitcast(FP8X4),
                        rhs_scale=x_bytes[:, a:b],
                        start=True,
                        stop=True,
                    )
                copy = nc.vector.tensor_copy if len(banks) == 3 and first == pieces[1][0] else nc.scalar.copy
                copy(out=y[:, first:end], in_=acc[:, : end - first])
            ys[block, q] = y

        def term(block, c, a, b, tag=None, into=None):
            q, d = divmod(c, 2)
            name = f"term{block}{c}_{a}"
            if into is None:
                into = keep.tile([P, b - a], F32, align_bytes=64, name=name, tag=tag or name)[:]
            nc.vector.tensor_tensor(
                out=into,
                in0=ys[block, q][:].indirect(pos_sb[d][:, a // PER_COLUMN : b // PER_COLUMN]),
                in1=corr_sb[c][:, a:b],
                op=ALU.mult,
            )
            return into

        def spent(c, s):
            return corr_sb[c][:, s * P : (s + 1) * P]

        def sum_turned(four, strips, bank, name):
            sums = bank_tile(bank, name)
            for i in range(strips):
                for c in range(4):
                    nc.tensor.matmul(
                        out=sums[:, i * P : (i + 1) * P],
                        lhsT=four[c][:, i * P : (i + 1) * P],
                        rhs=identity[:],
                        is_transpose=True,
                        start=(c == 0),
                        stop=(c == 3),
                    )
            return sums

        whole = slice(0, P)
        upper = slice(P, 2 * P)

        gather_words(*pieces[0], "x_codes0")
        gather_words(*pieces[1], "x_codes1")
        w00 = quantize_w(round_low(0, 0, scalar_cast), P, "low00")
        gather_words(*pieces[2], "w_low00")
        w10 = quantize_w(round_low(1, 0, nc.vector.tensor_copy, "word_table"), P, "low10")
        product(0, 0, w00, whole, (0, 1, 2))
        a0 = term(0, 0, 0, V)
        product(0, 1, w10, whole, (3, 0))
        g01 = round_low(0, 1, scalar_cast, "w_scales_low00")
        g11 = round_low(1, 1, scalar_cast, "w_scales_low10")
        a1 = term(0, 1, 0, V)
        w01 = quantize_w(g01, P, "low01")
        a2 = term(0, 2, 0, V, "w_scales_low00")
        product(1, 0, w01, whole, (1, 2))
        a3 = term(0, 3, 0, V)
        w11 = quantize_w(g11, P, "low11")
        product(1, 1, w11, whole, (3, 0))
        sums_a = sum_turned((a0, a1, a2, a3), 4, 3, "sums_a")
        w_high = [
            keep.tile([P, 2 * P * PACK], BF16, align_bytes=64, name=f"w_high{q}", tag=f"w_codes_low{q}1")
            for q in range(2)
        ]
        for q in range(2):
            for h in range(2):
                round_high(q, h)
        b0 = term(1, 0, 0, V, "w_scales_low10")
        b1 = term(1, 1, 0, V)
        wh0 = quantize_w(w_high[0], 2 * P, "high0")
        b2 = term(1, 2, 0, V, "w_codes_low01")
        wh1 = quantize_w(w_high[1], 2 * P, "high1")
        b3 = term(1, 3, 0, V, "w_codes_low11")
        product(2, 0, wh0, whole, (1, 2))
        product(2, 1, wh1, whole, (4, 5))
        product(3, 0, wh0, upper, (6, 7))
        product(3, 1, wh1, upper, (0, 1))
        sums_b = sum_turned((b0, b1, b2, b3), 4, 5, "sums_b")

        turned = keep.tile([P, V // P, PACK, P], F32, align_bytes=64, name="turned", tag="w_codes_high1")
        for h, sums in enumerate((sums_a, sums_b)):
            nc.scalar.activation(
                out=turned[:, :, 0:2, h * (P // 2) : (h + 1) * (P // 2)],
                in_=sums[:].rearrange("v (s g t) -> v s t g", s=V // P, t=2),
                func=ACT.Relu,
            )

        out_rows = out_0.rearrange("(p t) v -> p t v", t=PACK)
        out_codes = keep.tile([P, V], U32, align_bytes=64, name="out_codes")
        out_scales = keep.tile([P, V], U8, align_bytes=64, name="out_scales")
        out_words = out_1[0].rearrange("p c r -> p (c r)").bitcast(I32)

        def quantize_out(rounded, s0, s1):
            cols = slice(s0 * P, s1 * P)
            nc.vector.quantize_mx(
                out=out_codes[:, cols].bitcast(FP8X4),
                scales=out_scales[:, cols],
                in_=rounded.rearrange("p v t -> p (v t)"),
            )

        def rectify(t, s, sums):
            nc.scalar.activation(out=turned[:, s, t, :], in_=sums[:, :P], func=ACT.Relu)

        def add_turned(sums, weighted, c):
            nc.tensor.matmul(
                out=sums[:, :P], lhsT=weighted, rhs=identity[:], is_transpose=True, start=(c == 0), stop=(c == 3)
            )

        def unit(t, s0, banks):
            strips = range(len(banks))
            sums = [bank_tile(banks[i], f"sums{t}{s0 + i}") for i in strips]
            for c in range(4):
                into = spent(c + 2, s0 - 1) if s0 > 0 and c < 2 else None
                weighted = term(t, c, s0 * P, (s0 + len(banks)) * P, into=into)
                for i in strips:
                    add_turned(sums[i], weighted[:, i * P : (i + 1) * P], c)
            for i in strips:
                rectify(t, s0 + i, sums[i])

        def turn_back(s, slots, bank):
            back = bank_tile(bank, f"back{s}")[:].rearrange("p (t v) -> p t v", t=PACK)
            for t in range(slots):
                nc.tensor.transpose(back[:, t, :], turned[:, s, t, :], identity[:])
            result = keep.tile([P, PACK, P], F32, name=f"result{s}")
            return back, result

        def finish(s, bank, rounded):
            back, result = turn_back(s, PACK, bank)
            nc.scalar.copy(out=rounded, in_=back.rearrange("p t v -> p v t"))
            nc.scalar.copy(out=result[:], in_=back)
            nc.sync.dma_start(out=out_rows[:, :, s * P : (s + 1) * P], in_=result[:])

        rounded01 = keep.tile([P, 2 * P, PACK], BF16, align_bytes=64, name="rounded01", tag="rounded01")
        rounded2 = keep.tile([P, P, PACK], BF16, align_bytes=64, name="rounded2", tag="rounded2")
        unit(2, 0, (6, 7, 0))
        last_back, last_result = turn_back(3, 2, 4)
        nc.scalar.copy(out=last_result[:, 0:2, :], in_=last_back[:, 0:2, :])
        nc.sync.dma_start(out=out_rows[:, 0:2, 3 * P :], in_=last_result[:, 0:2, :])
        unit(3, 0, (3,))
        finish(0, 1, rounded01[:, :P, :])
        unit(3, 1, (5,))
        finish(1, 2, rounded01[:, P:, :])
        unit(3, 2, (3,))
        finish(2, 4, rounded2[:])

        def add(out, in0, in1):
            nc.vector.tensor_tensor(out=out, in0=in0, in1=in1, op=ALU.add)

        partial = keep.tile([P, 3, P], F32, name="partial")
        c0 = term(2, 0, 3 * P, V, into=spent(2, 2))
        c1 = term(2, 1, 3 * P, V, into=spent(3, 2))
        c2 = term(2, 2, 3 * P, V, into=spent(0, 1))
        add(partial[:, 0, :], c0, c1)
        c3 = term(2, 3, 3 * P, V, into=spent(1, 1))
        add(partial[:, 1, :], partial[:, 0, :], c2)
        d0 = term(3, 0, 3 * P, V, into=spent(1, 2))
        add(last_result[:, 2, :], partial[:, 1, :], c3)
        d1 = term(3, 1, 3 * P, V, into=spent(0, 2))
        d2 = term(3, 2, 3 * P, V)
        add(partial[:, 2, :], d0, d1)
        d3 = term(3, 3, 3 * P, V)
        quantize_out(rounded01[:], 0, 2)
        nc.sync.dma_start(out=out_words[:, : 2 * P], in_=out_codes[:, : 2 * P].bitcast(I32))
        triple = keep.tile([P, P], F32, align_bytes=64, name="triple", tag="rounded01")
        add(triple[:], partial[:, 2, :], d2)
        add(last_result[:, 3, :], triple[:], d3)
        quantize_out(rounded2[:], 2, 3)
        last = keep.tile([P, 2, P * PACK], BF16, align_bytes=64, name="last", tag="rounded2")
        last_rounded = last[:, 0, :].rearrange("p (v t) -> p v t", t=PACK)
        last_rows = last[:, 1, :].bitcast(F32).rearrange("p (t v) -> p t v", t=2)
        nc.vector.tensor_scalar_max(out=last_rounded, in0=last_result[:].rearrange("p t v -> p v t"), scalar1=0.0)
        nc.scalar.activation(out=last_rows, in_=last_result[:, 2:4, :], func=ACT.Relu)
        nc.scalar.dma_start(out=out_rows[:, 2:4, 3 * P :], in_=last_rows)
        quantize_out(last_rounded, 3, 4)
        nc.sync.dma_start(out=out_words[:, 2 * P :], in_=out_codes[:, 2 * P :].bitcast(I32))
        for quad in range(4):
            queue = nc.sync if quad < 2 else nc.scalar
            queue.dma_start(
                out=out_2[0, 4 * quad : 4 * quad + 4, :].bitcast(I32),
                in_=out_scales[32 * quad : 32 * quad + 4, :].bitcast(I32),
            )
